import numpy as np, ml_dtypes
CORES = [122,123,126,250,251,254,378,379,382,506,507,510]
N = 12
import mx_ref
NC, K, S = 128, 2, 2
CNT = [[0,28,0,0,28,28,16,12,0,4,0,12],[4,0,8,12,0,4,4,0,52,16,28,0],[0,36,0,16,0,20,8,28,16,4,0,0],[12,0,0,0,16,40,8,16,4,32,0,0],[4,0,0,40,0,24,0,4,0,24,28,4],[12,4,0,0,8,0,56,12,4,16,4,12],[8,28,48,0,0,4,0,16,4,0,8,12],[36,4,12,4,16,0,0,0,16,28,12,0],[0,0,12,40,16,0,0,8,0,0,16,36],[48,16,4,4,4,4,8,0,28,0,12,0],[4,0,8,0,28,4,28,0,0,4,0,52],[0,12,36,12,12,0,0,32,4,0,20,0]]
OFF = [[sum(c[:f]) for f in range(N + 1)] for c in CNT]
BF = ml_dtypes.bfloat16
def setup_inputs(rng):
    def f(*shape):
        return mx_ref.flush((rng.standard_normal(shape, dtype=np.float32) * np.exp2(rng.integers(-2, 3, shape[:-1] + (1,)))).astype(BF))
    return {"w": f(N, 128, 512), "x": f(N, 128, 4 * NC)}
def setup_inputs_blocks(rng):
    d = setup_inputs(rng)
    for k in ("w", "x"): d[k] = mx_ref.spread(d[k], rng, 1)
    return d
def setup_inputs_wide(rng):
    d = setup_inputs(rng)
    for k in ("x",): d[k] = mx_ref.flush((d[k].astype(np.float32) * np.exp2(rng.integers(-8, 9, (N, 1, 1))).astype(np.float32)).astype(BF))
    return d
def setup_inputs_zeros(rng):
    d = setup_inputs(rng); v = d["x"].reshape(N, 128, -1, 4).copy()
    v[np.broadcast_to((rng.random((N, 1, v.shape[2], 1)) < 0.33), v.shape)] = 0
    d["x"] = v.reshape(d["x"].shape)
    return d
def reference(w, x):
    y = np.zeros((N, 128, NC), np.float32)
    for k in range(K):
        for e in range(N):
            f = (e - S * k) % N
            t = np.concatenate([x[j][:, 4 * OFF[j][f]:4 * OFF[j][f + 1]] for j in range(N)], axis=1)
            p = mx_ref.matmul(mx_ref.quantize(w[e]), mx_ref.quantize(t)); c = 0
            for j in range(N):
                a, b = OFF[j][f], OFF[j][f + 1]
                y[j][:, a:b] = p[:, c:c + b - a] if k == 0 else y[j][:, a:b] + p[:, c:c + b - a]; c += b - a
    return {"y": y}

@@ -1,0 +1,246 @@
+from concourse.bass import DstId, RemoteDMATransfer
+from concourse.mybir import dt, AluOpType
+
+N = 12
+NC = 128
+SHIFT = 2
+BANK = 512
+NH = 4
+NP = 3
+OWN = NP - 1
+
+SCRATCH = {
+    "wbf": ("sbuf", [128, 4 * NC], "bfloat16"),
+    "xbf": ("sbuf", [128, 4 * NC], "bfloat16"),
+    "wq": ("sbuf", [128, NH * NC], "float8_e4m3fn_x4"),
+    "ws": ("sbuf", [128, NH * NC], "uint8"),
+    "xq": ("sbuf", [128, NP * NC], "float8_e4m3fn_x4"),
+    "xs": ("sbuf", [128, NP * NC], "uint8"),
+    "ps": ("psum", [128, 2 * NH * BANK], "float32"),
+    "stage": ("sbuf", [128, 2 * 2 * NC], "float32"),
+    "rin": ("sbuf", [128, 2 * 2 * NC], "float32"),
+    "ysb": ("sbuf", [128, NC], "float32"),
+}
+SEMAPHORES = (["ldw", "ldx", "qw", "qx", "ev", "st", "sent", "g0", "g1"]
+              + ["S%d" % k for k in range(NH)] + ["C%d" % k for k in range(NH)]
+              + ["MP%d" % k for k in range(NH)] + ["MO%d" % k for k in range(NH)]
+              + ["XS%d" % p for p in range(NP - 1)] + ["XC%d" % p for p in range(NP - 1)]
+              + ["A%d" % p for p in range(NP - 1)] + ["B%d" % p for p in range(NP - 1)])
+
+
+def _bits(mask):
+    return bin(mask).count("1")
+
+
+def _plan(cores, cnt, topo):
+    n = len(cores)
+
+    def one_chip(a, b):
+        return topo.host(cores[a]) == topo.host(cores[b]) and topo.chip(cores[a]) == topo.chip(cores[b])
+
+    peers = [[q for q in range(n) if q != r and one_chip(q, r)] for r in range(n)]
+    place = [sum(1 for q in peers[r] if q < r) for r in range(n)]
+    lane = [sum(1 for q in peers[r] if q < r and topo.die(cores[q]) == topo.die(cores[r])) for r in range(n)]
+    hosts = sorted({topo.host(c) for c in cores})
+    slot = [hosts.index(topo.host(c)) for c in cores]
+    near, far = [], []
+    for r in range(n):
+        twins = [q for q in range(n) if q != r and place[q] == place[r]]
+        t = [q for q in twins if topo.may_write(cores[r], cores[q])]
+        t.sort(key=lambda q: topo.rack(topo.host(cores[q])) == topo.rack(topo.host(cores[r])))
+        near.append(t[::-1] if lane[r] % 2 else t)
+        far.append([q for q in twins if not topo.may_write(cores[r], cores[q])][0])
+    first = [[sum(cnt[j][:f]) for f in range(n + 1)] for j in range(n)]
+    serve = [[(r, 0)] + [(e, 0) for k in (1, 0) for e in near[r] if near[e][k] == r] + [(far[r], 1)] for r in range(n)]
+    pieces = [[{q: [] for q in peers[r]} for _ in range(2)] for r in range(n)]
+    width = [[{q: 0 for q in peers[r]} for _ in range(2)] for r in range(n)]
+    for r in range(n):
+        for e, call in serve[r]:
+            for q in peers[r]:
+                for f in (e, (e - SHIFT) % n):
+                    if cnt[q][f]:
+                        pieces[r][call][q].append((e, f, first[q][f], first[q][f + 1], width[r][call][q]))
+                        width[r][call][q] += cnt[q][f]
+    return dict(peers=peers, place=place, slot=slot, near=near, far=far, first=first, serve=serve, pieces=pieces, width=width)
+
+
+def _windows(P, r, call):
+    qs = [q for q in P["peers"][r] if P["width"][r][call][q]]
+    base = call * 2 * NC
+    start, x = {}, base
+    for q in qs:
+        start[q] = x
+        x += P["width"][r][call][q]
+    wide = max([P["width"][r][call][q] for q in qs] + [0])
+    win = {q: (base if i == 0 else x - wide) for i, q in enumerate(qs)}
+    return qs, start, win, wide
+
+
+def rank_program(g, core, T, topo):
+    r = T.rank_of(core)
+    if r is None:
+        return
+    cores, cnt, sem = list(T.cores), T.tables["CNT"], T.sem
+    P = _plan(cores, cnt, topo)
+    peers, slot, near, far, first = P["peers"][r], P["slot"], P["near"], P["far"], P["first"]
+
+    def engines(s):
+        out = topo.mask(cores[s], cores[near[s][0]])
+        stay = topo.mask(cores[s], cores[P["peers"][s][0]]) & ~out
+        one = [1 << i for i in range(stay.bit_length()) if stay >> i & 1]
+        return out, stay, [sum(one[0::2]), sum(one[1::2])]
+
+    out, stay, half = engines(r)
+
+    def seat(at, guest):
+        return P["peers"][at].index(guest)
+
+    def tile(e):
+        return slice(slot[e] * NC, (slot[e] + 1) * NC)
+
+    def xcol(k):
+        return slice(k * NC, (k + 1) * NC)
+
+    def ids(qs):
+        res = []
+        for q in qs:
+            rid, pid = topo.addr(cores[q], core)
+            res.append(DstId(rid=rid, pnc=pid))
+        return res
+
+    g.sync.dma_start(T.wbf[:], T.w[:]).then_inc(sem.ldw, 16)
+    g.sync.dma_start(T.xbf[:], T.x[:]).then_inc(sem.ldx, 16)
+    g.vector.wait_ge(sem.ldw, 16)
+    g.vector.quantize_mx(T.wq[:, tile(r)], T.ws[:, tile(r)], T.wbf[:]).then_inc(sem.qw, 1)
+    g.vector.wait_ge(sem.ldx, 16)
+    g.vector.quantize_mx(T.xq[:, xcol(OWN)], T.xs[:, xcol(OWN)], T.xbf[:]).then_inc(sem.qx, 1)
+
+    sent = [0]
+
+    def w_part(part, e, q):
+        sent[0] += _bits(out)
+        if part == "S":
+            src, dst = T.ws[:, tile(e)], T.ws[:, tile(e)]
+        else:
+            src, dst = T.wq[:, tile(e)].bitcast(dt.uint8), T.wq[:, tile(e)].bitcast(dt.uint8)
+        return RemoteDMATransfer(dst_ids=ids([q]), dma_engine_mask=out, remote_sem=sem[part + str(slot[e])], src=src, dst=dst)
+
+    def x_parts(part):
+        res = []
+        for q, mask in zip(peers, half):
+            k = seat(q, r)
+            sent[0] += _bits(mask)
+            if part == "S":
+                src, dst = T.xs[:, xcol(OWN)], T.xs[:, xcol(k)]
+            else:
+                src, dst = T.xq[:, xcol(OWN)].bitcast(dt.uint8), T.xq[:, xcol(k)].bitcast(dt.uint8)
+            res.append(RemoteDMATransfer(dst_ids=ids([q]), dma_engine_mask=mask, remote_sem=sem["X" + part + str(k)], src=src, dst=dst))
+        return res
+
+    t1, t2 = near[r]
+    g.wait_ge(sem.qw, 1)
+    g.remote_dma_fused([w_part("C", r, t1)], local_sem=sem.sent)
+    g.wait_ge(sem.qx, 1)
+    g.remote_dma_fused([w_part("S", r, t2)] + x_parts("S"), local_sem=sem.sent)
+    g.remote_dma_fused([w_part("C", r, t2)] + x_parts("C"), local_sem=sem.sent)
+    g.remote_dma_fused([w_part("S", r, t1)], local_sem=sem.sent)
+    for part, k in (("C", 0), ("S", 1)):
+        for e in near[r]:
+            if near[e][k] == r:
+                g.wait_ge(sem[part + str(slot[e])], _bits(engines(e)[0]))
+                g.remote_dma_fused([w_part(part, e, far[e])], local_sem=sem.sent)
+
+    def have(e):
+        if e == r:
+            g.tensor.wait_ge(sem.qw, 1)
+        else:
+            g.tensor.wait_ge(sem["S%d" % slot[e]], _bits(out))
+            g.tensor.wait_ge(sem["C%d" % slot[e]], _bits(out))
+
+    def mm_own(e):
+        b = (NH + slot[e]) * BANK
+        g.tensor.matmul_mx(T.ps[:, b:b + NC], T.wq[:, tile(e)], T.ws[:, tile(e)],
+                           T.xq[:, xcol(OWN)], T.xs[:, xcol(OWN)], True, True).then_inc(sem["MO%d" % slot[e]], 1)
+
+    def mm_peers(e):
+        b = slot[e] * BANK
+        g.tensor.matmul_mx(T.ps[:, b:b + OWN * NC], T.wq[:, tile(e)], T.ws[:, tile(e)],
+                           T.xq[:, 0:OWN * NC], T.xs[:, 0:OWN * NC], True, True).then_inc(sem["MP%d" % slot[e]], 1)
+
+    early = [e for e, call in P["serve"][r] if call == 0]
+    late = [e for e, call in P["serve"][r] if call == 1]
+    g.tensor.wait_ge(sem.qx, 1)
+    for e in early:
+        have(e)
+        mm_own(e)
+    for q in peers:
+        k = seat(r, q)
+        n_eng = _bits(engines(q)[2][seat(q, r)])
+        g.tensor.wait_ge(sem["XS%d" % k], n_eng)
+        g.tensor.wait_ge(sem["XC%d" % k], n_eng)
+    for e in early:
+        mm_peers(e)
+    for e in late:
+        have(e)
+        mm_peers(e)
+        mm_own(e)
+
+    for call in range(2):
+        qs, start, win, wide = _windows(P, r, call)
+        n_pieces = 0
+        for e, c in P["serve"][r]:
+            if c != call:
+                continue
+            g.vector.wait_ge(sem["MP%d" % slot[e]], 1)
+            for q in qs:
+                for e2, f, a, b, o in P["pieces"][r][call][q]:
+                    if e2 == e:
+                        src = slot[e] * BANK + seat(r, q) * NC
+                        g.vector.tensor_copy(T.stage[:, start[q] + o:start[q] + o + b - a],
+                                             T.ps[:, src + a:src + b]).then_inc(sem["g%d" % call], 1)
+                        n_pieces += 1
+        if qs:
+            g.wait_ge(sem["g%d" % call], n_pieces)
+            trs = []
+            for q, mask in zip(qs, (out, stay)):
+                k = seat(q, r)
+                land = (k * 2 + call) * NC
+                trs.append(RemoteDMATransfer(dst_ids=ids([q]), dma_engine_mask=mask, remote_sem=sem["AB"[call] + str(k)],
+                                             src=T.stage[:, win[q]:win[q] + wide], dst=T.rin[:, land:land + wide]))
+                sent[0] += _bits(mask)
+            g.remote_dma_fused(trs, local_sem=sem.sent)
+
+    def slice_of(e, f):
+        a, b = first[r][f], first[r][f + 1]
+        srv = [s for s in [r] + peers if P["place"][s] == P["place"][e]][0]
+        call = [c for e2, c in P["serve"][srv] if e2 == e][0]
+        if srv == r:
+            src = (NH + slot[e]) * BANK
+            return call, T.ps[:, src + a:src + b], ("MO%d" % slot[e], 1)
+        qs, start, win, wide = _windows(P, srv, call)
+        o = [p[4] for p in P["pieces"][srv][call][r] if p[0] == e and p[1] == f][0]
+        k = seat(r, srv)
+        col = (k * 2 + call) * NC + start[r] + o - win[r]
+        return call, T.rin[:, col:col + b - a], ("AB"[call] + str(k), _bits(engines(srv)[qs.index(r)]))
+
+    jobs = []
+    for f in range(N):
+        if cnt[r][f]:
+            s1, s2 = slice_of(f, f), slice_of((f + SHIFT) % N, f)
+            jobs.append((max(s1[0], s2[0]), f, s1, s2))
+    jobs.sort(key=lambda j: (j[0], j[1]))
+    waited = set()
+    for _, f, s1, s2 in jobs:
+        for s in (s1, s2):
+            if s[2] not in waited:
+                waited.add(s[2])
+                g.vector.wait_ge(sem[s[2][0]], s[2][1])
+        g.vector.tensor_tensor(T.ysb[:, first[r][f]:first[r][f + 1]], s1[1], s2[1], AluOpType.add).then_inc(sem.ev, 1)
+    for k in range(NH):
+        if ("MO%d" % k, 1) not in waited:
+            g.vector.wait_ge(sem["MO%d" % k], 1)
+
+    g.sync.wait_ge(sem.ev, len(jobs))
+    g.sync.dma_start(T.y[:], T.ysb[:]).then_inc(sem.st, 16)
+    g.sync.wait_ge(sem.st, 16)
+    g.wait_ge(sem.sent, sent[0])

@@ -1,5 +1,5 @@
 from concourse.bass import DstId, RemoteDMATransfer
-from concourse.mybir import dt, AluOpType
+from concourse.mybir import dt, AluOpType, ActivationFunctionType
 
 N = 12
 NC = 128
@@ -8,6 +8,7 @@ BANK = 512
 NH = 4
 NP = 3
 OWN = NP - 1
+WORLD = 512
 
 SCRATCH = {
     "wbf": ("sbuf", [128, 4 * NC], "bfloat16"),
@@ -17,15 +18,17 @@ SCRATCH = {
     "xq": ("sbuf", [128, NP * NC], "float8_e4m3fn_x4"),
     "xs": ("sbuf", [128, NP * NC], "uint8"),
     "ps": ("psum", [128, 2 * NH * BANK], "float32"),
-    "stage": ("sbuf", [128, 2 * 2 * NC], "float32"),
-    "rin": ("sbuf", [128, 2 * 2 * NC], "float32"),
+    "stage": ("sbuf", [128, 2 * NC], "float32"),
+    "rin": ("sbuf", [128, 2 * NC], "float32"),
     "ysb": ("sbuf", [128, NC], "float32"),
 }
-SEMAPHORES = (["ldw", "ldx", "qw", "qx", "ev", "st", "sent", "g0", "g1"]
+SEMAPHORES = (["ldw", "ldx", "qw", "qx", "ev", "st", "sent", "g0"]
               + ["S%d" % k for k in range(NH)] + ["C%d" % k for k in range(NH)]
               + ["MP%d" % k for k in range(NH)] + ["MO%d" % k for k in range(NH)]
               + ["XS%d" % p for p in range(NP - 1)] + ["XC%d" % p for p in range(NP - 1)]
-              + ["A%d" % p for p in range(NP - 1)] + ["B%d" % p for p in range(NP - 1)])
+              + ["A%d" % p for p in range(NP - 1)])
+
+_CACHE = {}
 
 
 def _bits(mask):
@@ -36,57 +39,99 @@ def _plan(cores, cnt, topo):
     n = len(cores)
 
     def one_chip(a, b):
-        return topo.host(cores[a]) == topo.host(cores[b]) and topo.chip(cores[a]) == topo.chip(cores[b])
+        return topo.host(a) == topo.host(b) and topo.chip(a) == topo.chip(b)
 
-    peers = [[q for q in range(n) if q != r and one_chip(q, r)] for r in range(n)]
+    peers = [[q for q in range(n) if q != r and one_chip(cores[q], cores[r])] for r in range(n)]
     place = [sum(1 for q in peers[r] if q < r) for r in range(n)]
     lane = [sum(1 for q in peers[r] if q < r and topo.die(cores[q]) == topo.die(cores[r])) for r in range(n)]
     hosts = sorted({topo.host(c) for c in cores})
     slot = [hosts.index(topo.host(c)) for c in cores]
-    near, far = [], []
+    near, far, helper = [], [], []
     for r in range(n):
         twins = [q for q in range(n) if q != r and place[q] == place[r]]
         t = [q for q in twins if topo.may_write(cores[r], cores[q])]
         t.sort(key=lambda q: topo.rack(topo.host(cores[q])) == topo.rack(topo.host(cores[r])))
         near.append(t[::-1] if lane[r] % 2 else t)
         far.append([q for q in twins if not topo.may_write(cores[r], cores[q])][0])
+        idle = [c for c in range(WORLD) if c not in cores and one_chip(c, cores[r]) and topo.die(c) == topo.die(cores[r])]
+        helper.append(idle[lane[r]])
+    via = [[e for e in near[r] if near[e][0] == r][0] for r in range(n)]
+    direct = [[e for e in near[r] if near[e][1] == r][0] for r in range(n)]
     first = [[sum(cnt[j][:f]) for f in range(n + 1)] for j in range(n)]
-    serve = [[(r, 0)] + [(e, 0) for k in (1, 0) for e in near[r] if near[e][k] == r] + [(far[r], 1)] for r in range(n)]
-    pieces = [[{q: [] for q in peers[r]} for _ in range(2)] for r in range(n)]
-    width = [[{q: 0 for q in peers[r]} for _ in range(2)] for r in range(n)]
+    serve = [[r, via[r], far[r], direct[r]] for r in range(n)]
+    pieces = [{q: [] for q in peers[r]} for r in range(n)]
+    width = [{q: 0 for q in peers[r]} for r in range(n)]
     for r in range(n):
-        for e, call in serve[r]:
+        for e in serve[r]:
             for q in peers[r]:
                 for f in (e, (e - SHIFT) % n):
                     if cnt[q][f]:
-                        pieces[r][call][q].append((e, f, first[q][f], first[q][f + 1], width[r][call][q]))
-                        width[r][call][q] += cnt[q][f]
-    return dict(peers=peers, place=place, slot=slot, near=near, far=far, first=first, serve=serve, pieces=pieces, width=width)
+                        pieces[r][q].append((e, f, first[q][f], first[q][f + 1], width[r][q]))
+                        width[r][q] += cnt[q][f]
+    return dict(peers=peers, place=place, slot=slot, near=near, far=far, helper=helper, via=via, direct=direct,
+                first=first, serve=serve, pieces=pieces, width=width)
 
 
-def _windows(P, r, call):
-    qs = [q for q in P["peers"][r] if P["width"][r][call][q]]
-    base = call * 2 * NC
-    start, x = {}, base
+def _windows(P, r):
+    qs = [q for q in P["peers"][r] if P["width"][r][q]]
+    start, x = {}, 0
     for q in qs:
         start[q] = x
-        x += P["width"][r][call][q]
-    wide = max([P["width"][r][call][q] for q in qs] + [0])
-    win = {q: (base if i == 0 else x - wide) for i, q in enumerate(qs)}
+        x += P["width"][r][q]
+    wide = max([P["width"][r][q] for q in qs] + [0])
+    win = {q: (0 if i == 0 else x - wide) for i, q in enumerate(qs)}
     return qs, start, win, wide
 
 
 def rank_program(g, core, T, topo):
-    r = T.rank_of(core)
-    if r is None:
-        return
     cores, cnt, sem = list(T.cores), T.tables["CNT"], T.sem
-    P = _plan(cores, cnt, topo)
-    peers, slot, near, far, first = P["peers"][r], P["slot"], P["near"], P["far"], P["first"]
+    if "P" not in _CACHE:
+        _CACHE["P"] = _plan(cores, cnt, topo)
+    P = _CACHE["P"]
+    slot, near, far, first = P["slot"], P["near"], P["far"], P["first"]
+    r = T.rank_of(core)
+    if r is None and core not in P["helper"]:
+        return
+
+    def tile(e):
+        return slice(slot[e] * NC, (slot[e] + 1) * NC)
+
+    def ids(cs):
+        res = []
+        for c in cs:
+            rid, pid = topo.addr(c, core)
+            res.append(DstId(rid=rid, pnc=pid))
+        return res
+
+    sent = [0]
+
+    def w_part(part, e, dst_core, mask):
+        sent[0] += _bits(mask)
+        if part == "S":
+            src, dst = T.ws[:, tile(e)], T.ws[:, tile(e)]
+        else:
+            src, dst = T.wq[:, tile(e)].bitcast(dt.uint8), T.wq[:, tile(e)].bitcast(dt.uint8)
+        return RemoteDMATransfer(dst_ids=ids([dst_core]), dma_engine_mask=mask, remote_sem=sem[part + str(slot[e])], src=src, dst=dst)
+
+    def split(c, away, home):
+        out = topo.mask(c, away)
+        return out, topo.mask(c, home) & ~out
+
+    if r is None:
+        s = P["helper"].index(core)
+        e = P["via"][s]
+        h_out, h_stay = split(core, cores[far[e]], cores[s])
+        n_in = _bits(topo.mask(cores[e], core))
+        for part in ("S", "C"):
+            g.wait_ge(sem[part + str(slot[e])], n_in)
+            g.remote_dma_fused([w_part(part, e, cores[far[e]], h_out), w_part(part, e, cores[s], h_stay)], local_sem=sem.sent)
+        g.wait_ge(sem.sent, sent[0])
+        return
+
+    peers = P["peers"][r]
 
     def engines(s):
-        out = topo.mask(cores[s], cores[near[s][0]])
-        stay = topo.mask(cores[s], cores[P["peers"][s][0]]) & ~out
+        out, stay = split(cores[s], cores[near[s][0]], cores[P["peers"][s][0]])
         one = [1 << i for i in range(stay.bit_length()) if stay >> i & 1]
         return out, stay, [sum(one[0::2]), sum(one[1::2])]
 
@@ -95,35 +140,15 @@ def rank_program(g, core, T, topo):
     def seat(at, guest):
         return P["peers"][at].index(guest)
 
-    def tile(e):
-        return slice(slot[e] * NC, (slot[e] + 1) * NC)
-
     def xcol(k):
         return slice(k * NC, (k + 1) * NC)
 
-    def ids(qs):
-        res = []
-        for q in qs:
-            rid, pid = topo.addr(cores[q], core)
-            res.append(DstId(rid=rid, pnc=pid))
-        return res
-
     g.sync.dma_start(T.wbf[:], T.w[:]).then_inc(sem.ldw, 16)
-    g.sync.dma_start(T.xbf[:], T.x[:]).then_inc(sem.ldx, 16)
+    g.scalar.dma_start(T.xbf[:], T.x[:]).then_inc(sem.ldx, 16)
     g.vector.wait_ge(sem.ldw, 16)
     g.vector.quantize_mx(T.wq[:, tile(r)], T.ws[:, tile(r)], T.wbf[:]).then_inc(sem.qw, 1)
     g.vector.wait_ge(sem.ldx, 16)
     g.vector.quantize_mx(T.xq[:, xcol(OWN)], T.xs[:, xcol(OWN)], T.xbf[:]).then_inc(sem.qx, 1)
-
-    sent = [0]
-
-    def w_part(part, e, q):
-        sent[0] += _bits(out)
-        if part == "S":
-            src, dst = T.ws[:, tile(e)], T.ws[:, tile(e)]
-        else:
-            src, dst = T.wq[:, tile(e)].bitcast(dt.uint8), T.wq[:, tile(e)].bitcast(dt.uint8)
-        return RemoteDMATransfer(dst_ids=ids([q]), dma_engine_mask=out, remote_sem=sem[part + str(slot[e])], src=src, dst=dst)
 
     def x_parts(part):
         res = []
@@ -134,28 +159,29 @@ def rank_program(g, core, T, topo):
                 src, dst = T.xs[:, xcol(OWN)], T.xs[:, xcol(k)]
             else:
                 src, dst = T.xq[:, xcol(OWN)].bitcast(dt.uint8), T.xq[:, xcol(k)].bitcast(dt.uint8)
-            res.append(RemoteDMATransfer(dst_ids=ids([q]), dma_engine_mask=mask, remote_sem=sem["X" + part + str(k)], src=src, dst=dst))
+            res.append(RemoteDMATransfer(dst_ids=ids([cores[q]]), dma_engine_mask=mask, remote_sem=sem["X" + part + str(k)], src=src, dst=dst))
         return res
 
     t1, t2 = near[r]
     g.wait_ge(sem.qw, 1)
-    g.remote_dma_fused([w_part("C", r, t1)], local_sem=sem.sent)
     g.wait_ge(sem.qx, 1)
-    g.remote_dma_fused([w_part("S", r, t2)] + x_parts("S"), local_sem=sem.sent)
-    g.remote_dma_fused([w_part("C", r, t2)] + x_parts("C"), local_sem=sem.sent)
-    g.remote_dma_fused([w_part("S", r, t1)], local_sem=sem.sent)
-    for part, k in (("C", 0), ("S", 1)):
-        for e in near[r]:
-            if near[e][k] == r:
-                g.wait_ge(sem[part + str(slot[e])], _bits(engines(e)[0]))
-                g.remote_dma_fused([w_part(part, e, far[e])], local_sem=sem.sent)
+    g.remote_dma_fused([w_part("S", r, P["helper"][t1], out)] + x_parts("S"), local_sem=sem.sent)
+    g.remote_dma_fused([w_part("C", r, P["helper"][t1], out)] + x_parts("C"), local_sem=sem.sent)
+    g.remote_dma_fused([w_part("S", r, cores[t2], out)], local_sem=sem.sent)
+    g.remote_dma_fused([w_part("C", r, cores[t2], out)], local_sem=sem.sent)
+
+    def landed(e):
+        if e == P["direct"][r]:
+            return _bits(topo.mask(cores[e], core))
+        h = P["helper"][r] if e == P["via"][r] else P["helper"][near[e][0]]
+        return _bits(split(h, cores[far[e]], cores[near[e][0]])[1 if e == P["via"][r] else 0])
 
     def have(e):
         if e == r:
             g.tensor.wait_ge(sem.qw, 1)
         else:
-            g.tensor.wait_ge(sem["S%d" % slot[e]], _bits(out))
-            g.tensor.wait_ge(sem["C%d" % slot[e]], _bits(out))
+            g.tensor.wait_ge(sem["S%d" % slot[e]], landed(e))
+            g.tensor.wait_ge(sem["C%d" % slot[e]], landed(e))
 
     def mm_own(e):
         b = (NH + slot[e]) * BANK
@@ -167,8 +193,7 @@ def rank_program(g, core, T, topo):
         g.tensor.matmul_mx(T.ps[:, b:b + OWN * NC], T.wq[:, tile(e)], T.ws[:, tile(e)],
                            T.xq[:, 0:OWN * NC], T.xs[:, 0:OWN * NC], True, True).then_inc(sem["MP%d" % slot[e]], 1)
 
-    early = [e for e, call in P["serve"][r] if call == 0]
-    late = [e for e, call in P["serve"][r] if call == 1]
+    early, late = P["serve"][r][:-1], P["serve"][r][-1:]
     g.tensor.wait_ge(sem.qx, 1)
     for e in early:
         have(e)
@@ -185,62 +210,65 @@ def rank_program(g, core, T, topo):
         mm_peers(e)
         mm_own(e)
 
-    for call in range(2):
-        qs, start, win, wide = _windows(P, r, call)
-        n_pieces = 0
-        for e, c in P["serve"][r]:
-            if c != call:
-                continue
-            g.vector.wait_ge(sem["MP%d" % slot[e]], 1)
-            for q in qs:
-                for e2, f, a, b, o in P["pieces"][r][call][q]:
-                    if e2 == e:
-                        src = slot[e] * BANK + seat(r, q) * NC
-                        g.vector.tensor_copy(T.stage[:, start[q] + o:start[q] + o + b - a],
-                                             T.ps[:, src + a:src + b]).then_inc(sem["g%d" % call], 1)
-                        n_pieces += 1
-        if qs:
-            g.wait_ge(sem["g%d" % call], n_pieces)
-            trs = []
-            for q, mask in zip(qs, (out, stay)):
-                k = seat(q, r)
-                land = (k * 2 + call) * NC
-                trs.append(RemoteDMATransfer(dst_ids=ids([q]), dma_engine_mask=mask, remote_sem=sem["AB"[call] + str(k)],
-                                             src=T.stage[:, win[q]:win[q] + wide], dst=T.rin[:, land:land + wide]))
-                sent[0] += _bits(mask)
-            g.remote_dma_fused(trs, local_sem=sem.sent)
+    qs, start, win, wide = _windows(P, r)
+    n_pieces = 0
+    for i, e in enumerate(P["serve"][r]):
+        by_scalar = i % 2 == 0
+        (g.scalar if by_scalar else g.vector).wait_ge(sem["MP%d" % slot[e]], 1)
+        for q in qs:
+            for e2, f, a, b, o in P["pieces"][r][q]:
+                if e2 == e:
+                    src = slot[e] * BANK + seat(r, q) * NC
+                    dst_ap, src_ap = T.stage[:, start[q] + o:start[q] + o + b - a], T.ps[:, src + a:src + b]
+                    if by_scalar:
+                        g.scalar.activation(dst_ap, src_ap, ActivationFunctionType.Copy).then_inc(sem.g0, 1)
+                    else:
+                        g.vector.tensor_copy(dst_ap, src_ap).then_inc(sem.g0, 1)
+                    n_pieces += 1
+    g.wait_ge(sem.g0, n_pieces)
+    trs = []
+    for q, mask in zip(qs, (out, stay)):
+        k = seat(q, r)
+        trs.append(RemoteDMATransfer(dst_ids=ids([cores[q]]), dma_engine_mask=mask, remote_sem=sem["A" + str(k)],
+                                     src=T.stage[:, win[q]:win[q] + wide], dst=T.rin[:, k * NC:k * NC + wide]))
+        sent[0] += _bits(mask)
+    g.remote_dma_fused(trs, local_sem=sem.sent)
 
     def slice_of(e, f):
         a, b = first[r][f], first[r][f + 1]
         srv = [s for s in [r] + peers if P["place"][s] == P["place"][e]][0]
-        call = [c for e2, c in P["serve"][srv] if e2 == e][0]
         if srv == r:
             src = (NH + slot[e]) * BANK
-            return call, T.ps[:, src + a:src + b], ("MO%d" % slot[e], 1)
-        qs, start, win, wide = _windows(P, srv, call)
-        o = [p[4] for p in P["pieces"][srv][call][r] if p[0] == e and p[1] == f][0]
+            return T.ps[:, src + a:src + b], ("MO%d" % slot[e], 1)
+        qs2, start2, win2, _ = _windows(P, srv)
+        o = [p[4] for p in P["pieces"][srv][r] if p[0] == e and p[1] == f][0]
         k = seat(r, srv)
-        col = (k * 2 + call) * NC + start[r] + o - win[r]
-        return call, T.rin[:, col:col + b - a], ("AB"[call] + str(k), _bits(engines(srv)[qs.index(r)]))
+        col = k * NC + start2[r] + o - win2[r]
+        return T.rin[:, col:col + b - a], ("A" + str(k), _bits(engines(srv)[qs2.index(r)]))
 
-    jobs = []
-    for f in range(N):
-        if cnt[r][f]:
-            s1, s2 = slice_of(f, f), slice_of((f + SHIFT) % N, f)
-            jobs.append((max(s1[0], s2[0]), f, s1, s2))
-    jobs.sort(key=lambda j: (j[0], j[1]))
     waited = set()
-    for _, f, s1, s2 in jobs:
+    n_jobs = 0
+    for f in range(N):
+        if not cnt[r][f]:
+            continue
+        s1, s2 = slice_of(f, f), slice_of((f + SHIFT) % N, f)
         for s in (s1, s2):
-            if s[2] not in waited:
-                waited.add(s[2])
-                g.vector.wait_ge(sem[s[2][0]], s[2][1])
-        g.vector.tensor_tensor(T.ysb[:, first[r][f]:first[r][f + 1]], s1[1], s2[1], AluOpType.add).then_inc(sem.ev, 1)
+            if s[1] not in waited:
+                waited.add(s[1])
+                g.vector.wait_ge(sem[s[1][0]], s[1][1])
+        g.vector.tensor_tensor(T.ysb[:, first[r][f]:first[r][f + 1]], s1[0], s2[0], AluOpType.add).then_inc(sem.ev, 1)
+        n_jobs += 1
     for k in range(NH):
         if ("MO%d" % k, 1) not in waited:
             g.vector.wait_ge(sem["MO%d" % k], 1)
+    for q in peers:
+        qs2 = _windows(P, q)[0]
+        if r in qs2:
+            key = ("A" + str(seat(r, q)), _bits(engines(q)[qs2.index(r)]))
+            if key not in waited:
+                g.vector.wait_ge(sem[key[0]], key[1])
 
-    g.sync.wait_ge(sem.ev, len(jobs))
+    g.sync.wait_ge(sem.ev, n_jobs)
     g.sync.dma_start(T.y[:], T.ysb[:]).then_inc(sem.st, 16)
     g.sync.wait_ge(sem.st, 16)
     g.wait_ge(sem.sent, sent[0])

from concourse.bass import DstId, RemoteDMATransfer
from concourse.mybir import dt, AluOpType, ActivationFunctionType

N = 12
NC = 128
SHIFT = 2
BANK = 512
NH = 4
NP = 3
OWN = NP - 1
WORLD = 512

SCRATCH = {
    "wbf": ("sbuf", [128, 4 * NC], "bfloat16"),
    "xbf": ("sbuf", [128, 4 * NC], "bfloat16"),
    "wq": ("sbuf", [128, NH * NC], "float8_e4m3fn_x4"),
    "ws": ("sbuf", [128, NH * NC], "uint8"),
    "xq": ("sbuf", [128, NP * NC], "float8_e4m3fn_x4"),
    "xs": ("sbuf", [128, NP * NC], "uint8"),
    "ps": ("psum", [128, 2 * NH * BANK], "float32"),
    "stage": ("sbuf", [128, 2 * NC], "float32"),
    "rin": ("sbuf", [128, 2 * NC], "float32"),
    "ysb": ("sbuf", [128, NC], "float32"),
}
SEMAPHORES = (["ldw", "ldx", "qw", "qx", "ev", "st", "sent", "g0"]
              + ["S%d" % k for k in range(NH)] + ["C%d" % k for k in range(NH)]
              + ["MP%d" % k for k in range(NH)] + ["MO%d" % k for k in range(NH)]
              + ["XS%d" % p for p in range(NP - 1)] + ["XC%d" % p for p in range(NP - 1)]
              + ["A%d" % p for p in range(NP - 1)])

_CACHE = {}


def _bits(mask):
    return bin(mask).count("1")


def _plan(cores, cnt, topo):
    n = len(cores)

    def one_chip(a, b):
        return topo.host(a) == topo.host(b) and topo.chip(a) == topo.chip(b)

    peers = [[q for q in range(n) if q != r and one_chip(cores[q], cores[r])] for r in range(n)]
    place = [sum(1 for q in peers[r] if q < r) for r in range(n)]
    lane = [sum(1 for q in peers[r] if q < r and topo.die(cores[q]) == topo.die(cores[r])) for r in range(n)]
    hosts = sorted({topo.host(c) for c in cores})
    slot = [hosts.index(topo.host(c)) for c in cores]
    near, far, helper = [], [], []
    for r in range(n):
        twins = [q for q in range(n) if q != r and place[q] == place[r]]
        t = [q for q in twins if topo.may_write(cores[r], cores[q])]
        t.sort(key=lambda q: topo.rack(topo.host(cores[q])) == topo.rack(topo.host(cores[r])))
        near.append(t[::-1] if lane[r] % 2 else t)
        far.append([q for q in twins if not topo.may_write(cores[r], cores[q])][0])
        idle = [c for c in range(WORLD) if c not in cores and one_chip(c, cores[r]) and topo.die(c) == topo.die(cores[r])]
        helper.append(idle[lane[r]])
    via = [[e for e in near[r] if near[e][0] == r][0] for r in range(n)]
    direct = [[e for e in near[r] if near[e][1] == r][0] for r in range(n)]
    first = [[sum(cnt[j][:f]) for f in range(n + 1)] for j in range(n)]
    serve = [[r, via[r], far[r], direct[r]] for r in range(n)]
    pieces = [{q: [] for q in peers[r]} for r in range(n)]
    width = [{q: 0 for q in peers[r]} for r in range(n)]
    for r in range(n):
        for e in serve[r]:
            for q in peers[r]:
                for f in (e, (e - SHIFT) % n):
                    if cnt[q][f]:
                        pieces[r][q].append((e, f, first[q][f], first[q][f + 1], width[r][q]))
                        width[r][q] += cnt[q][f]
    return dict(peers=peers, place=place, slot=slot, near=near, far=far, helper=helper, via=via, direct=direct,
                first=first, serve=serve, pieces=pieces, width=width)


def _windows(P, r):
    qs = [q for q in P["peers"][r] if P["width"][r][q]]
    start, x = {}, 0
    for q in qs:
        start[q] = x
        x += P["width"][r][q]
    wide = max([P["width"][r][q] for q in qs] + [0])
    win = {q: (0 if i == 0 else x - wide) for i, q in enumerate(qs)}
    return qs, start, win, wide


def rank_program(g, core, T, topo):
    cores, cnt, sem = list(T.cores), T.tables["CNT"], T.sem
    if "P" not in _CACHE:
        _CACHE["P"] = _plan(cores, cnt, topo)
    P = _CACHE["P"]
    slot, near, far, first = P["slot"], P["near"], P["far"], P["first"]
    r = T.rank_of(core)
    if r is None and core not in P["helper"]:
        return

    def tile(e):
        return slice(slot[e] * NC, (slot[e] + 1) * NC)

    def ids(cs):
        res = []
        for c in cs:
            rid, pid = topo.addr(c, core)
            res.append(DstId(rid=rid, pnc=pid))
        return res

    sent = [0]

    def w_part(part, e, dst_core, mask):
        sent[0] += _bits(mask)
        if part == "S":
            src, dst = T.ws[:, tile(e)], T.ws[:, tile(e)]
        else:
            src, dst = T.wq[:, tile(e)].bitcast(dt.uint8), T.wq[:, tile(e)].bitcast(dt.uint8)
        return RemoteDMATransfer(dst_ids=ids([dst_core]), dma_engine_mask=mask, remote_sem=sem[part + str(slot[e])], src=src, dst=dst)

    def split(c, away, home):
        out = topo.mask(c, away)
        return out, topo.mask(c, home) & ~out

    if r is None:
        s = P["helper"].index(core)
        e = P["via"][s]
        h_out, h_stay = split(core, cores[far[e]], cores[s])
        n_in = _bits(topo.mask(cores[e], core))
        for part in ("S", "C"):
            g.wait_ge(sem[part + str(slot[e])], n_in)
            g.remote_dma_fused([w_part(part, e, cores[far[e]], h_out), w_part(part, e, cores[s], h_stay)], local_sem=sem.sent)
        g.wait_ge(sem.sent, sent[0])
        return

    peers = P["peers"][r]

    def engines(s):
        out, stay = split(cores[s], cores[near[s][0]], cores[P["peers"][s][0]])
        one = [1 << i for i in range(stay.bit_length()) if stay >> i & 1]
        return out, stay, [sum(one[0::2]), sum(one[1::2])]

    out, stay, half = engines(r)

    def seat(at, guest):
        return P["peers"][at].index(guest)

    def xcol(k):
        return slice(k * NC, (k + 1) * NC)

    g.sync.dma_start(T.wbf[:], T.w[:]).then_inc(sem.ldw, 16)
    g.scalar.dma_start(T.xbf[:], T.x[:]).then_inc(sem.ldx, 16)
    g.vector.wait_ge(sem.ldw, 16)
    g.vector.quantize_mx(T.wq[:, tile(r)], T.ws[:, tile(r)], T.wbf[:]).then_inc(sem.qw, 1)
    g.vector.wait_ge(sem.ldx, 16)
    g.vector.quantize_mx(T.xq[:, xcol(OWN)], T.xs[:, xcol(OWN)], T.xbf[:]).then_inc(sem.qx, 1)

    def x_parts(part):
        res = []
        for q, mask in zip(peers, half):
            k = seat(q, r)
            sent[0] += _bits(mask)
            if part == "S":
                src, dst = T.xs[:, xcol(OWN)], T.xs[:, xcol(k)]
            else:
                src, dst = T.xq[:, xcol(OWN)].bitcast(dt.uint8), T.xq[:, xcol(k)].bitcast(dt.uint8)
            res.append(RemoteDMATransfer(dst_ids=ids([cores[q]]), dma_engine_mask=mask, remote_sem=sem["X" + part + str(k)], src=src, dst=dst))
        return res

    t1, t2 = near[r]
    g.wait_ge(sem.qw, 1)
    g.wait_ge(sem.qx, 1)
    g.remote_dma_fused([w_part("S", r, P["helper"][t1], out)] + x_parts("S"), local_sem=sem.sent)
    g.remote_dma_fused([w_part("C", r, P["helper"][t1], out)] + x_parts("C"), local_sem=sem.sent)
    g.remote_dma_fused([w_part("S", r, cores[t2], out)], local_sem=sem.sent)
    g.remote_dma_fused([w_part("C", r, cores[t2], out)], local_sem=sem.sent)

    def landed(e):
        if e == P["direct"][r]:
            return _bits(topo.mask(cores[e], core))
        h = P["helper"][r] if e == P["via"][r] else P["helper"][near[e][0]]
        return _bits(split(h, cores[far[e]], cores[near[e][0]])[1 if e == P["via"][r] else 0])

    def have(e):
        if e == r:
            g.tensor.wait_ge(sem.qw, 1)
        else:
            g.tensor.wait_ge(sem["S%d" % slot[e]], landed(e))
            g.tensor.wait_ge(sem["C%d" % slot[e]], landed(e))

    def mm_own(e):
        b = (NH + slot[e]) * BANK
        g.tensor.matmul_mx(T.ps[:, b:b + NC], T.wq[:, tile(e)], T.ws[:, tile(e)],
                           T.xq[:, xcol(OWN)], T.xs[:, xcol(OWN)], True, True).then_inc(sem["MO%d" % slot[e]], 1)

    def mm_peers(e):
        b = slot[e] * BANK
        g.tensor.matmul_mx(T.ps[:, b:b + OWN * NC], T.wq[:, tile(e)], T.ws[:, tile(e)],
                           T.xq[:, 0:OWN * NC], T.xs[:, 0:OWN * NC], True, True).then_inc(sem["MP%d" % slot[e]], 1)

    early, late = P["serve"][r][:-1], P["serve"][r][-1:]
    g.tensor.wait_ge(sem.qx, 1)
    for e in early:
        have(e)
        mm_own(e)
    for q in peers:
        k = seat(r, q)
        n_eng = _bits(engines(q)[2][seat(q, r)])
        g.tensor.wait_ge(sem["XS%d" % k], n_eng)
        g.tensor.wait_ge(sem["XC%d" % k], n_eng)
    for e in early:
        mm_peers(e)
    for e in late:
        have(e)
        mm_peers(e)
        mm_own(e)

    qs, start, win, wide = _windows(P, r)
    n_pieces = 0
    for i, e in enumerate(P["serve"][r]):
        by_scalar = i % 2 == 0
        (g.scalar if by_scalar else g.vector).wait_ge(sem["MP%d" % slot[e]], 1)
        for q in qs:
            for e2, f, a, b, o in P["pieces"][r][q]:
                if e2 == e:
                    src = slot[e] * BANK + seat(r, q) * NC
                    dst_ap, src_ap = T.stage[:, start[q] + o:start[q] + o + b - a], T.ps[:, src + a:src + b]
                    if by_scalar:
                        g.scalar.activation(dst_ap, src_ap, ActivationFunctionType.Copy).then_inc(sem.g0, 1)
                    else:
                        g.vector.tensor_copy(dst_ap, src_ap).then_inc(sem.g0, 1)
                    n_pieces += 1
    g.wait_ge(sem.g0, n_pieces)
    trs = []
    for q, mask in zip(qs, (out, stay)):
        k = seat(q, r)
        trs.append(RemoteDMATransfer(dst_ids=ids([cores[q]]), dma_engine_mask=mask, remote_sem=sem["A" + str(k)],
                                     src=T.stage[:, win[q]:win[q] + wide], dst=T.rin[:, k * NC:k * NC + wide]))
        sent[0] += _bits(mask)
    g.remote_dma_fused(trs, local_sem=sem.sent)

    def slice_of(e, f):
        a, b = first[r][f], first[r][f + 1]
        srv = [s for s in [r] + peers if P["place"][s] == P["place"][e]][0]
        if srv == r:
            src = (NH + slot[e]) * BANK
            return T.ps[:, src + a:src + b], ("MO%d" % slot[e], 1)
        qs2, start2, win2, _ = _windows(P, srv)
        o = [p[4] for p in P["pieces"][srv][r] if p[0] == e and p[1] == f][0]
        k = seat(r, srv)
        col = k * NC + start2[r] + o - win2[r]
        return T.rin[:, col:col + b - a], ("A" + str(k), _bits(engines(srv)[qs2.index(r)]))

    waited = set()
    n_jobs = 0
    for f in range(N):
        if not cnt[r][f]:
            continue
        s1, s2 = slice_of(f, f), slice_of((f + SHIFT) % N, f)
        for s in (s1, s2):
            if s[1] not in waited:
                waited.add(s[1])
                g.vector.wait_ge(sem[s[1][0]], s[1][1])
        g.vector.tensor_tensor(T.ysb[:, first[r][f]:first[r][f + 1]], s1[0], s2[0], AluOpType.add).then_inc(sem.ev, 1)
        n_jobs += 1
    for k in range(NH):
        if ("MO%d" % k, 1) not in waited:
            g.vector.wait_ge(sem["MO%d" % k], 1)
    for q in peers:
        qs2 = _windows(P, q)[0]
        if r in qs2:
            key = ("A" + str(seat(r, q)), _bits(engines(q)[qs2.index(r)]))
            if key not in waited:
                g.vector.wait_ge(sem[key[0]], key[1])

    g.sync.wait_ge(sem.ev, n_jobs)
    g.sync.dma_start(T.y[:], T.ysb[:]).then_inc(sem.st, 16)
    g.sync.wait_ge(sem.st, 16)
    g.wait_ge(sem.sent, sent[0])
